import numpy as np
import ml_dtypes


def mxq(x, axis, fmt="e4m3"):
    dtype, down = {"e4m3": (ml_dtypes.float8_e4m3fn, 7), "e5m2": (ml_dtypes.float8_e5m2, 14)}[fmt]
    v = np.moveaxis(np.asarray(x, np.float32).astype(ml_dtypes.bfloat16).astype(np.float64), axis, -1)
    blocks = v.reshape(v.shape[:-1] + (-1, 32))
    amax = np.abs(blocks).max(-1, keepdims=True)
    byte = np.maximum(np.where(amax > 0, np.frexp(amax)[1] - 1 + 127, 0) - down, 1)
    scale = np.exp2(byte - 127.0)
    codes = (blocks / scale).astype(np.float32).astype(dtype).astype(np.float64)
    return np.moveaxis((codes * scale).reshape(v.shape), -1, axis)


WIDE = False


def mx_kscale(k):
    if not WIDE:
        return np.ones(k)
    levels = np.array([10, -10, 5, -5, 0])
    if k % 512:
        return np.exp2(np.random.permutation(np.resize(levels, k // 32))).repeat(32)
    a = np.empty((k // 512, 16))
    for p in range(k // 512):
        a[p, :8] = np.random.permutation(np.resize(levels, 8))
        for g in range(8):
            far = levels[np.abs(levels - a[p, g]) >= 10]
            a[p, g + 8] = far[np.random.randint(len(far))]
    return np.exp2(a.ravel()).repeat(32)


def f64(x):
    return np.asarray(x).astype(np.float64)


def striped(idx):
    return np.tile(idx.reshape(-1, 16).T, (8, 1)).astype(np.uint16)


def unstriped(offs):
    return offs[:16].T.reshape(-1).astype(np.int64)


def striped8(idx):
    return np.concatenate([x.reshape(-1, 16).T for x in idx]).astype(np.uint16)


def runs(offs, k):
    lists = np.stack([offs[16 * r : 16 * r + 16].T.reshape(-1) for r in range(8)]).astype(np.int64)
    return lists[np.arange(k) % 512 // 64]


def pack_weight(w):
    k, n = w.shape
    w = f64(np.asarray(w, np.float32).astype(ml_dtypes.bfloat16)).reshape(k // 32, 32, n)
    amax = np.abs(w).max(1)
    byte = np.clip(np.where(amax > 0, np.frexp(amax)[1] - 1 + 127 - 7, 1), 1, 254)
    scaled = (w * np.exp2(127.0 - byte)[:, None, :]).reshape(k, n).astype(np.float32)
    words = np.ascontiguousarray(scaled.reshape(k // 512, 128, 4, n).transpose(0, 1, 3, 2)).astype(ml_dtypes.float8_e4m3fn).view(np.uint8)
    return words, np.ascontiguousarray(byte.astype(np.uint8).reshape(k // 512, 16, n))


def unpack_weight(words, scales):
    g, p, n, _ = words.shape
    vals = np.ascontiguousarray(words).view(ml_dtypes.float8_e4m3fn).astype(np.float64) * np.repeat(np.exp2(scales.astype(np.float64) - 127.0), 8, axis=1)[..., None]
    return vals.transpose(0, 1, 3, 2).reshape(g * 512, n)


def sigmoid(v):
    return 1.0 / (1.0 + np.exp(-np.maximum(v, -700.0)))

def planes(y):
    n, m = y.shape
    v = y.astype(np.float32).astype(ml_dtypes.bfloat16).astype(np.float64).reshape(n // 32, 32, m)
    top = np.abs(v).max(1)
    byte = np.clip(np.where(top > 0, np.frexp(top)[1] - 1 + 127 - 7, 1), 1, 254)
    codes = (v * np.exp2(127.0 - byte)[:, None, :]).reshape(n, m).astype(np.float32).astype(ml_dtypes.float8_e4m3fn).view(np.uint8)
    words = codes.reshape(n // 512, 128, 4, m).transpose(0, 1, 3, 2)
    return np.ascontiguousarray(words), np.ascontiguousarray(byte.astype(np.uint8).reshape(n // 512, 16, m))


K, T, S, G, H, C = 512, 1024, 512, 2048, 512, 512


def setup_inputs():
    n = np.random.standard_normal
    s = mx_kscale(K)[:, None]
    packed_xT = pack_weight(n((K, T)) * s)
    packed_dT = pack_weight(n((K, G)) / s)
    return {
        "x_words": packed_xT[0],
        "x_scales": packed_xT[1],
        "d_words": packed_dT[0],
        "d_scales": packed_dT[1],
        "gs": (np.random.uniform(0.5, 1.5, (K, 1)) / s).astype(np.float32),
        "offs": striped(np.random.permutation(T)[:S]),
        "k1": striped8(np.random.randint(0, G, (8, H))),
        "n1": striped8(np.stack([np.random.permutation(S) for _ in range(8)])),
        "n2": striped8(np.stack([np.random.permutation(S) for _ in range(8)])),
        "cand": striped(np.random.permutation(T)[:C]),
        "n3": striped8(np.stack([np.random.permutation(S) for _ in range(8)])),
        "n4": striped8(np.stack([np.random.permutation(S) for _ in range(8)])),
    }


def reference(x_words, x_scales, d_words, d_scales, gs, offs, k1, n1, n2, cand, n3, n4):
    x_cand = unpack_weight(x_words, x_scales)[:, unstriped(cand)]
    d_k1 = unpack_weight(d_words, d_scales)[np.arange(K)[:, None], runs(k1, K)]
    xq = unpack_weight(x_words, x_scales)[:, unstriped(offs)]
    h = 0.0625 * (d_k1.T @ xq)
    z = f64(gs) * (np.maximum(h * (sigmoid(h[np.arange(H)[:, None], runs(n1, H)])), h[np.arange(H)[:, None], runs(n2, H)]))
    s = 0.0625 * ((x_cand.T @ mxq(z, 0, "e4m3")))
    ex = np.exp(s)
    out_0 = np.log(ex + ex[np.arange(C)[:, None], runs(n3, C)]) - (s[np.arange(C)[:, None], runs(n4, C)])
    return (out_0,) + planes(out_0)

@@ -1,0 +1,204 @@
+from contextlib import ExitStack
+
+import concourse.mybir as mybir
+
+F32 = mybir.dt.float32
+BF16 = mybir.dt.bfloat16
+U32 = mybir.dt.uint32
+I32 = mybir.dt.int32
+U16 = mybir.dt.uint16
+U8 = mybir.dt.uint8
+FP8X4 = mybir.dt.float8_e4m3fn_x4
+ACT = mybir.ActivationFunctionType
+ALU = mybir.AluOpType
+
+P = 128
+PACK = 4
+T, G, N = 1024, 2048, 512
+HALF = 256
+LIST_COLS = N // 16
+FLOPS = 2 * 2 * 512 * 512 * 512
+
+
+def tile_picked_pqcgmaxlse_none_po_kernel(
+    tc, x_words, x_scales, d_words, d_scales, gs, offs, k1, n1, n2, cand, n3, n4, out_0, out_1, out_2
+):
+    nc = tc.nc
+    with ExitStack() as ctx:
+        keep = ctx.enter_context(tc.tile_pool(name="keep", bufs=1))
+        psum = ctx.enter_context(tc.psum_pool(name="psum", bufs=1))
+
+        def new(shape, dtype, name):
+            return keep.tile(shape, dtype, name=name, align_bytes=64)
+
+        def load_list(src, name):
+            tile = keep.tile([P, LIST_COLS], U16, name=name)
+            nc.sync.dma_start(tile[:], src)
+            return tile
+
+        def load_scale_rows(src, width, name):
+            tile = new([P, width], U8, name)
+            rows = src[0].bitcast(I32).unsqueeze(1).broadcast_to([16, 8, width // 4])
+            nc.sync.dma_start(tile[:].bitcast(I32), rows)
+            return tile
+
+        def load_words(src, width, name):
+            tile = new([P, width], I32, name)
+            nc.sync.dma_start(tile[:], src[0].rearrange("p n t -> p (n t)").bitcast(I32))
+            return tile
+
+        def place_scale_rows(dst, src):
+            for r in range(4):
+                queue = nc.sync if r % 2 == 0 else nc.scalar
+                queue.dma_start(dst[r:P:32, :].bitcast(I32), src[8 * r : P : 32, :].bitcast(I32))
+
+        def deal(dst, src):
+            nc.vector.tensor_copy(
+                dst.rearrange("p (t m) -> p t m", t=PACK), src.rearrange("p (m t) -> p t m", t=PACK)
+            )
+
+        def half_of(lst, c):
+            return lst[:, c * (HALF // 16) : (c + 1) * (HALF // 16)]
+
+        def weave_views(woven, planes):
+            return (
+                woven.rearrange("p (c i t) -> p c t i", i=4, t=PACK),
+                planes.rearrange("p t (c i) -> p c t i", i=4),
+            )
+
+        d_scale_tab = load_scale_rows(d_scales, G, "d_scale_tab")
+        k1_list = load_list(k1, "k1_list")
+        x_scale_tab = load_scale_rows(x_scales, T, "x_scale_tab")
+        offs_list = load_list(offs, "offs_list")
+        x_word_tab = load_words(x_words, T, "x_word_tab")
+        d_word_tab = load_words(d_words, G, "d_word_tab")
+        cand_list = load_list(cand, "cand_list")
+        n1_list = load_list(n1, "n1_list")
+        n2_list = load_list(n2, "n2_list")
+        gain = new([P, PACK], F32, "gain")
+        nc.sync.dma_start(gain[:], gs.rearrange("(p t) o -> p (t o)", t=PACK))
+        n3_list = load_list(n3, "n3_list")
+        n4_list = load_list(n4, "n4_list")
+
+        first_placed = new([P, 2 * N], U8, "first_placed")
+        nc.gpsimd.memset(first_placed[:].bitcast(I32), 0)
+        cand_placed = new([P, N], U8, "cand_placed")
+        nc.gpsimd.memset(cand_placed[:].bitcast(I32), 0)
+
+        first_picked = new([P, 2 * N], U8, "first_picked")
+        nc.vector.tensor_copy(first_picked[:, 0:N], d_scale_tab[:].indirect(k1_list[:]))
+        nc.vector.tensor_copy(first_picked[:, N : 2 * N], x_scale_tab[:].indirect(offs_list[:]))
+        place_scale_rows(first_placed, first_picked)
+        tok_words = new([P, N], U32, "tok_words")
+        nc.vector.tensor_copy(tok_words[:], x_word_tab[:].bitcast(U32).indirect(offs_list[:]))
+        dict_picked = new([P, N], U32, "dict_picked")
+        nc.vector.tensor_copy(dict_picked[:], d_word_tab[:].bitcast(U32).indirect(k1_list[:]))
+        dict_words = new([P, N], U32, "dict_words")
+        deal(dict_words[:], dict_picked[:])
+        dict_scales = new([P, N], U8, "dict_scales")
+        deal(dict_scales[:], first_placed[:, 0:N])
+
+        h = []
+        for t in range(PACK):
+            cols = slice(t * P, (t + 1) * P)
+            bank = psum.tile([P, N], F32, name=f"h_bank{t}")
+            nc.tensor.matmul_mx(
+                out=bank[:],
+                lhsT=dict_words[:, cols].bitcast(FP8X4),
+                lhsT_scale=dict_scales[:, cols],
+                rhs=tok_words[:].bitcast(FP8X4),
+                rhs_scale=first_placed[:, N : 2 * N],
+                start=True,
+                stop=True,
+            )
+            h_t = new([P, N], F32, f"h{t}")
+            nc.scalar.activation(h_t[:], bank[:], ACT.Copy, scale=0.0625)
+            h.append(h_t)
+
+        cand_scale_picked = new([P, N], U8, "cand_scale_picked")
+        nc.vector.tensor_copy(cand_scale_picked[:], x_scale_tab[:].indirect(cand_list[:]))
+        place_scale_rows(cand_placed, cand_scale_picked)
+        cand_picked = new([P, N], U32, "cand_picked")
+        nc.vector.tensor_copy(cand_picked[:], x_word_tab[:].bitcast(U32).indirect(cand_list[:]))
+        cand_words = new([P, N], U32, "cand_words")
+        deal(cand_words[:], cand_picked[:])
+        cand_scales = new([P, N], U8, "cand_scales")
+        deal(cand_scales[:], cand_placed[:])
+
+        ex = [new([P, N], F32, f"ex{t}") for t in range(PACK)]
+        neg_s = [new([P, N], F32, f"neg_s{t}") for t in range(PACK)]
+        ex_again = new([P, PACK, N], F32, "ex_again")
+        for c in range(N // HALF):
+            cols = slice(c * HALF, (c + 1) * HALF)
+            z_planes = new([P, PACK, HALF], BF16, f"z_planes{c}")
+            for t in range(PACK):
+                gate = new([P, HALF], F32, f"gate{c}{t}")
+                nc.scalar.activation(gate[:], h[t][:].indirect(half_of(n1_list, c)), ACT.Sigmoid)
+                other = new([P, HALF], F32, f"other{c}{t}")
+                nc.vector.tensor_copy(other[:], h[t][:].indirect(half_of(n2_list, c)))
+                gated = new([P, HALF], F32, f"gated{c}{t}")
+                nc.vector.tensor_tensor(gated[:], h[t][:, cols], gate[:], ALU.mult)
+                larger = new([P, HALF], F32, f"larger{c}{t}")
+                nc.vector.tensor_tensor(larger[:], gated[:], other[:], ALU.max)
+                nc.scalar.activation(z_planes[:, t, :], larger[:], ACT.Copy, scale=gain[:, t : t + 1])
+            z_woven = new([P, PACK * HALF], BF16, f"z_woven{c}")
+            dst, src = weave_views(z_woven[:], z_planes[:])
+            nc.vector.tensor_copy(dst, src)
+            z_words = new([P, HALF], U32, f"z_words{c}")
+            z_scales = new([P, HALF], U8, f"z_scales{c}")
+            nc.vector.quantize_mx(out=z_words[:].bitcast(FP8X4), scales=z_scales[:], in_=z_woven[:])
+            for pair in range(2):
+                bank = psum.tile([P, 2, HALF], F32, name=f"s_bank{c}{pair}")
+                for u in range(2):
+                    t = 2 * pair + u
+                    rows = slice(t * P, (t + 1) * P)
+                    nc.tensor.matmul_mx(
+                        out=bank[:, u, :],
+                        lhsT=cand_words[:, rows].bitcast(FP8X4),
+                        lhsT_scale=cand_scales[:, rows],
+                        rhs=z_words[:].bitcast(FP8X4),
+                        rhs_scale=z_scales[:],
+                        start=True,
+                        stop=True,
+                    )
+                for u in range(2):
+                    nc.scalar.activation(ex[2 * pair + u][:, cols], bank[:, u, :], ACT.Exp, scale=0.0625)
+                nc.scalar.activation(ex_again[:, 2 * pair : 2 * pair + 2, cols], bank[:], ACT.Exp, scale=0.0625)
+                for u in range(2):
+                    nc.scalar.activation(neg_s[2 * pair + u][:, cols], bank[:, u, :], ACT.Copy, scale=-0.0625)
+
+        log_sum = []
+        for t in range(PACK):
+            pair_sum = new([P, N], F32, f"pair_sum{t}")
+            for c in range(N // HALF):
+                cols = slice(c * HALF, (c + 1) * HALF)
+                nc.vector.tensor_tensor(
+                    pair_sum[:, cols], ex[t][:].indirect(half_of(n3_list, c)), ex_again[:, t, cols], ALU.add
+                )
+            log_t = new([P, N], F32, f"log_sum{t}")
+            nc.scalar.activation(log_t[:], pair_sum[:], ACT.Ln)
+            log_sum.append(log_t)
+
+        out_rows = out_0.rearrange("(p t) j -> p t j", t=PACK)
+        out_words = out_1[0].rearrange("p n t -> p (n t)").bitcast(I32)
+        y_scales = new([P, N], U8, "y_scales")
+        for c in range(N // HALF):
+            cols = slice(c * HALF, (c + 1) * HALF)
+            y = new([P, PACK, HALF], F32, f"y{c}")
+            for t in range(PACK):
+                nc.vector.tensor_tensor(
+                    y[:, t, :], neg_s[t][:].indirect(half_of(n4_list, c)), log_sum[t][:, cols], ALU.add
+                )
+            nc.sync.dma_start(out_rows[:, :, cols], y[:])
+            y_woven = new([P, PACK * HALF], BF16, f"y_woven{c}")
+            dst, src = weave_views(y_woven[:], y[:])
+            if c == 0:
+                nc.scalar.copy(dst, src)
+            else:
+                nc.vector.tensor_copy(dst, src)
+            y_words = new([P, HALF], U32, f"y_words{c}")
+            nc.vector.quantize_mx(out=y_words[:].bitcast(FP8X4), scales=y_scales[:, cols], in_=y_woven[:])
+            nc.sync.dma_start(out_words[:, cols], y_words[:].bitcast(I32))
+        for r in range(4):
+            queue = nc.sync if r % 2 == 0 else nc.scalar
+            queue.dma_start(out_2[0].bitcast(I32)[r:16:4, :], y_scales[r:P:32, :].bitcast(I32))

@@ -28,8 +28,8 @@ def tile_picked_pqcgmaxlse_none_po_kernel(
         keep = ctx.enter_context(tc.tile_pool(name="keep", bufs=1))
         psum = ctx.enter_context(tc.psum_pool(name="psum", bufs=1))
 
-        def new(shape, dtype, name):
-            return keep.tile(shape, dtype, name=name, align_bytes=64)
+        def new(shape, dtype, name, tag=""):
+            return keep.tile(shape, dtype, name=name, tag=tag, align_bytes=64)
 
         def load_list(src, name):
             tile = keep.tile([P, LIST_COLS], U16, name=name)
@@ -47,14 +47,15 @@ def tile_picked_pqcgmaxlse_none_po_kernel(
             nc.sync.dma_start(tile[:], src[0].rearrange("p n t -> p (n t)").bitcast(I32))
             return tile
 
-        def place_scale_rows(dst, src):
-            for r in range(4):
-                queue = nc.sync if r % 2 == 0 else nc.scalar
-                queue.dma_start(dst[r:P:32, :].bitcast(I32), src[8 * r : P : 32, :].bitcast(I32))
+        def place_scale_rows(queue, dst, src):
+            for q in range(4):
+                queue.dma_start(
+                    dst[32 * q : 32 * q + 4, :].bitcast(I32), src[32 * q : 32 * q + 32 : 8, :].bitcast(I32)
+                )
 
         def deal(dst, src):
             nc.vector.tensor_copy(
-                dst.rearrange("p (t m) -> p t m", t=PACK), src.rearrange("p (m t) -> p t m", t=PACK)
+                dst.rearrange("p (t m) -> p m t", t=PACK), src.rearrange("p (m t) -> p m t", t=PACK)
             )
 
         def half_of(lst, c):
@@ -66,10 +67,10 @@ def tile_picked_pqcgmaxlse_none_po_kernel(
                 planes.rearrange("p t (c i) -> p c t i", i=4),
             )
 
-        d_scale_tab = load_scale_rows(d_scales, G, "d_scale_tab")
-        k1_list = load_list(k1, "k1_list")
         x_scale_tab = load_scale_rows(x_scales, T, "x_scale_tab")
         offs_list = load_list(offs, "offs_list")
+        d_scale_tab = load_scale_rows(d_scales, G, "d_scale_tab")
+        k1_list = load_list(k1, "k1_list")
         x_word_tab = load_words(x_words, T, "x_word_tab")
         d_word_tab = load_words(d_words, G, "d_word_tab")
         cand_list = load_list(cand, "cand_list")
@@ -80,68 +81,87 @@ def tile_picked_pqcgmaxlse_none_po_kernel(
         n3_list = load_list(n3, "n3_list")
         n4_list = load_list(n4, "n4_list")
 
-        first_placed = new([P, 2 * N], U8, "first_placed")
-        nc.gpsimd.memset(first_placed[:].bitcast(I32), 0)
-        cand_placed = new([P, N], U8, "cand_placed")
-        nc.gpsimd.memset(cand_placed[:].bitcast(I32), 0)
+        warm = new([P, 1], F32, "warm")
+        nc.vector.memset(warm[:], 0.0)
+        warm_out = new([P, 1], F32, "warm_out")
+        nc.scalar.activation(warm_out[:], warm[:], ACT.Sigmoid)
 
-        first_picked = new([P, 2 * N], U8, "first_picked")
-        nc.vector.tensor_copy(first_picked[:, 0:N], d_scale_tab[:].indirect(k1_list[:]))
-        nc.vector.tensor_copy(first_picked[:, N : 2 * N], x_scale_tab[:].indirect(offs_list[:]))
-        place_scale_rows(first_placed, first_picked)
+        first_scales = new([P, 2 * N], U8, "first_scales")
+        nc.vector.memset(first_scales[:].bitcast(I32), 0)
+        cand_scales = new([P, N], U8, "cand_scales")
+        nc.vector.memset(cand_scales[:].bitcast(I32), 0)
+
+        tok_scale_picked = new([P, N], U8, "tok_scale_picked")
+        nc.vector.tensor_copy(tok_scale_picked[:], x_scale_tab[:].indirect(offs_list[:]))
+        dict_scale_picked = new([P, N], U8, "dict_scale_picked")
+        nc.vector.tensor_copy(dict_scale_picked[:], d_scale_tab[:].indirect(k1_list[:]))
+        first_staged = new([P, 2 * N], U8, "first_staged", tag="slot_b")
+        nc.vector.tensor_copy(first_staged[:, N : 2 * N].bitcast(I32), tok_scale_picked[:].bitcast(I32))
+        deal(first_staged[:, 0:N], dict_scale_picked[:])
+        place_scale_rows(nc.scalar, first_scales, first_staged)
         tok_words = new([P, N], U32, "tok_words")
         nc.vector.tensor_copy(tok_words[:], x_word_tab[:].bitcast(U32).indirect(offs_list[:]))
-        dict_picked = new([P, N], U32, "dict_picked")
+        dict_picked = new([P, N], U32, "dict_picked", tag="slot_a")
         nc.vector.tensor_copy(dict_picked[:], d_word_tab[:].bitcast(U32).indirect(k1_list[:]))
         dict_words = new([P, N], U32, "dict_words")
         deal(dict_words[:], dict_picked[:])
-        dict_scales = new([P, N], U8, "dict_scales")
-        deal(dict_scales[:], first_placed[:, 0:N])
 
         h = []
+        gate = {}
         for t in range(PACK):
             cols = slice(t * P, (t + 1) * P)
             bank = psum.tile([P, N], F32, name=f"h_bank{t}")
             nc.tensor.matmul_mx(
                 out=bank[:],
                 lhsT=dict_words[:, cols].bitcast(FP8X4),
-                lhsT_scale=dict_scales[:, cols],
+                lhsT_scale=first_scales[:, cols],
                 rhs=tok_words[:].bitcast(FP8X4),
-                rhs_scale=first_placed[:, N : 2 * N],
+                rhs_scale=first_scales[:, N : 2 * N],
                 start=True,
                 stop=True,
             )
             h_t = new([P, N], F32, f"h{t}")
             nc.scalar.activation(h_t[:], bank[:], ACT.Copy, scale=0.0625)
             h.append(h_t)
+            gate[0, t] = new([P, HALF], F32, f"gate0{t}")
+            nc.scalar.activation(gate[0, t][:], h_t[:].indirect(half_of(n1_list, 0)), ACT.Sigmoid)
+        for t in range(PACK):
+            gate[1, t] = new([P, HALF], F32, f"gate1{t}")
+            nc.scalar.activation(gate[1, t][:], h[t][:].indirect(half_of(n1_list, 1)), ACT.Sigmoid)
 
-        cand_scale_picked = new([P, N], U8, "cand_scale_picked")
+        cand_scale_picked = new([P, N], U8, "cand_scale_picked", tag="slot_a")
         nc.vector.tensor_copy(cand_scale_picked[:], x_scale_tab[:].indirect(cand_list[:]))
-        place_scale_rows(cand_placed, cand_scale_picked)
-        cand_picked = new([P, N], U32, "cand_picked")
+        cand_picked = new([P, N], U32, "cand_picked", tag="slot_b")
         nc.vector.tensor_copy(cand_picked[:], x_word_tab[:].bitcast(U32).indirect(cand_list[:]))
+        cand_staged = new([P, N], U8, "cand_staged")
+        deal(cand_staged[:], cand_scale_picked[:])
+        place_scale_rows(nc.sync, cand_scales, cand_staged)
         cand_words = new([P, N], U32, "cand_words")
         deal(cand_words[:], cand_picked[:])
-        cand_scales = new([P, N], U8, "cand_scales")
-        deal(cand_scales[:], cand_placed[:])
 
         ex = [new([P, N], F32, f"ex{t}") for t in range(PACK)]
         neg_s = [new([P, N], F32, f"neg_s{t}") for t in range(PACK)]
-        ex_again = new([P, PACK, N], F32, "ex_again")
+        ex_again = [new([P, PACK, HALF], F32, f"ex_again{c}") for c in range(2)]
+        s_bank = {}
         for c in range(N // HALF):
             cols = slice(c * HALF, (c + 1) * HALF)
-            z_planes = new([P, PACK, HALF], BF16, f"z_planes{c}")
-            for t in range(PACK):
-                gate = new([P, HALF], F32, f"gate{c}{t}")
-                nc.scalar.activation(gate[:], h[t][:].indirect(half_of(n1_list, c)), ACT.Sigmoid)
-                other = new([P, HALF], F32, f"other{c}{t}")
-                nc.vector.tensor_copy(other[:], h[t][:].indirect(half_of(n2_list, c)))
-                gated = new([P, HALF], F32, f"gated{c}{t}")
-                nc.vector.tensor_tensor(gated[:], h[t][:, cols], gate[:], ALU.mult)
-                larger = new([P, HALF], F32, f"larger{c}{t}")
-                nc.vector.tensor_tensor(larger[:], gated[:], other[:], ALU.max)
-                nc.scalar.activation(z_planes[:, t, :], larger[:], ACT.Copy, scale=gain[:, t : t + 1])
-            z_woven = new([P, PACK * HALF], BF16, f"z_woven{c}")
+            z_planes = new([P, PACK, HALF], BF16, f"z_planes{c}", tag="slot_c" if c == 0 else "")
+            other_head = new([P, HALF], F32, f"other_head{c}")
+            other_rest = new([P, PACK - 1, HALF], F32, f"other_rest{c}", tag="slot_c" if c == 1 else "")
+            gated_head = new([P, HALF], F32, f"gated_head{c}")
+            gated_rest = new([P, PACK - 1, HALF], F32, f"gated_rest{c}", tag="slot_d" if c == 1 else "")
+            other = [other_head[:]] + [other_rest[:, t, :] for t in range(PACK - 1)]
+            gated = [gated_head[:]] + [gated_rest[:, t, :] for t in range(PACK - 1)]
+            for t in range(PACK + 1):
+                if t < PACK:
+                    nc.vector.tensor_tensor(gated[t], h[t][:, cols], gate[c, t][:], ALU.mult)
+                if t > 0:
+                    larger = new([P, HALF], F32, f"larger{c}{t}")
+                    nc.vector.tensor_tensor(larger[:], gated[t - 1], other[t - 1], ALU.max)
+                    nc.scalar.activation(z_planes[:, t - 1, :], larger[:], ACT.Copy, scale=gain[:, t - 1 : t])
+                if t < PACK:
+                    nc.vector.tensor_copy(other[t], h[t][:].indirect(half_of(n2_list, c)))
+            z_woven = new([P, PACK * HALF], BF16, f"z_woven{c}", tag="slot_d" if c == 0 else "")
             dst, src = weave_views(z_woven[:], z_planes[:])
             nc.vector.tensor_copy(dst, src)
             z_words = new([P, HALF], U32, f"z_words{c}")
@@ -149,6 +169,7 @@ def tile_picked_pqcgmaxlse_none_po_kernel(
             nc.vector.quantize_mx(out=z_words[:].bitcast(FP8X4), scales=z_scales[:], in_=z_woven[:])
             for pair in range(2):
                 bank = psum.tile([P, 2, HALF], F32, name=f"s_bank{c}{pair}")
+                s_bank[c, pair] = bank
                 for u in range(2):
                     t = 2 * pair + u
                     rows = slice(t * P, (t + 1) * P)
@@ -162,22 +183,28 @@ def tile_picked_pqcgmaxlse_none_po_kernel(
                         stop=True,
                     )
                 for u in range(2):
-                    nc.scalar.activation(ex[2 * pair + u][:, cols], bank[:, u, :], ACT.Exp, scale=0.0625)
-                nc.scalar.activation(ex_again[:, 2 * pair : 2 * pair + 2, cols], bank[:], ACT.Exp, scale=0.0625)
-                for u in range(2):
-                    nc.scalar.activation(neg_s[2 * pair + u][:, cols], bank[:, u, :], ACT.Copy, scale=-0.0625)
+                    t = 2 * pair + u
+                    nc.scalar.activation(ex[t][:, cols], bank[:, u, :], ACT.Exp, scale=0.0625)
+                    if c == 0:
+                        nc.sync.dma_start(ex_again[c][:, t, :], ex[t][:, cols])
+                    else:
+                        nc.vector.tensor_copy(ex_again[c][:, t, :], ex[t][:, cols])
+
+        for c in range(N // HALF):
+            cols = slice(c * HALF, (c + 1) * HALF)
+            for t in range(PACK):
+                nc.scalar.activation(neg_s[t][:, cols], s_bank[c, t // 2][:, t % 2, :], ACT.Copy, scale=-0.0625)
 
         log_sum = []
-        for t in range(PACK):
-            pair_sum = new([P, N], F32, f"pair_sum{t}")
-            for c in range(N // HALF):
-                cols = slice(c * HALF, (c + 1) * HALF)
+        for c in range(N // HALF):
+            pair_sum = new([P, PACK, HALF], F32, f"pair_sum{c}")
+            for t in range(PACK):
                 nc.vector.tensor_tensor(
-                    pair_sum[:, cols], ex[t][:].indirect(half_of(n3_list, c)), ex_again[:, t, cols], ALU.add
+                    pair_sum[:, t, :], ex[t][:].indirect(half_of(n3_list, c)), ex_again[c][:, t, :], ALU.add
                 )
-            log_t = new([P, N], F32, f"log_sum{t}")
-            nc.scalar.activation(log_t[:], pair_sum[:], ACT.Ln)
-            log_sum.append(log_t)
+            log_c = new([P, PACK, HALF], F32, f"log_sum{c}")
+            nc.scalar.activation(log_c[:], pair_sum[:], ACT.Ln)
+            log_sum.append(log_c)
 
         out_rows = out_0.rearrange("(p t) j -> p t j", t=PACK)
         out_words = out_1[0].rearrange("p n t -> p (n t)").bitcast(I32)
@@ -187,7 +214,7 @@ def tile_picked_pqcgmaxlse_none_po_kernel(
             y = new([P, PACK, HALF], F32, f"y{c}")
             for t in range(PACK):
                 nc.vector.tensor_tensor(
-                    y[:, t, :], neg_s[t][:].indirect(half_of(n4_list, c)), log_sum[t][:, cols], ALU.add
+                    y[:, t, :], neg_s[t][:].indirect(half_of(n4_list, c)), log_sum[c][:, t, :], ALU.add
                 )
             nc.sync.dma_start(out_rows[:, :, cols], y[:])
             y_woven = new([P, PACK * HALF], BF16, f"y_woven{c}")
@@ -199,6 +226,8 @@ def tile_picked_pqcgmaxlse_none_po_kernel(
             y_words = new([P, HALF], U32, f"y_words{c}")
             nc.vector.quantize_mx(out=y_words[:].bitcast(FP8X4), scales=y_scales[:, cols], in_=y_woven[:])
             nc.sync.dma_start(out_words[:, cols], y_words[:].bitcast(I32))
-        for r in range(4):
-            queue = nc.sync if r % 2 == 0 else nc.scalar
-            queue.dma_start(out_2[0].bitcast(I32)[r:16:4, :], y_scales[r:P:32, :].bitcast(I32))
+        for q in range(4):
+            queue = nc.sync if q % 2 == 0 else nc.scalar
+            queue.dma_start(
+                out_2[0].bitcast(I32)[4 * q : 4 * q + 4, :], y_scales[32 * q : 32 * q + 4, :].bitcast(I32)
+            )

@@ -16,6 +16,9 @@ P = 128
 PACK = 4
 T, G, N = 1024, 2048, 512
 HALF = 256
+WIDE = 2 * N
+Z_CHUNKS = (slice(0, 256), slice(256, 512))
+Y_CHUNKS = (slice(0, 256), slice(256, 384), slice(384, 512))
 LIST_COLS = N // 16
 FLOPS = 2 * 2 * 512 * 512 * 512
 
@@ -58,8 +61,8 @@ def tile_picked_pqcgmaxlse_none_po_kernel(
                 dst.rearrange("p (t m) -> p m t", t=PACK), src.rearrange("p (m t) -> p m t", t=PACK)
             )
 
-        def half_of(lst, c):
-            return lst[:, c * (HALF // 16) : (c + 1) * (HALF // 16)]
+        def entries(lst, cols):
+            return lst[:, cols.start // 16 : cols.stop // 16]
 
         def weave_views(woven, planes):
             return (
@@ -123,11 +126,16 @@ def tile_picked_pqcgmaxlse_none_po_kernel(
             h_t = new([P, N], F32, f"h{t}")
             nc.scalar.activation(h_t[:], bank[:], ACT.Copy, scale=0.0625)
             h.append(h_t)
-            gate[0, t] = new([P, HALF], F32, f"gate0{t}")
-            nc.scalar.activation(gate[0, t][:], h_t[:].indirect(half_of(n1_list, 0)), ACT.Sigmoid)
-        for t in range(PACK):
-            gate[1, t] = new([P, HALF], F32, f"gate1{t}")
-            nc.scalar.activation(gate[1, t][:], h[t][:].indirect(half_of(n1_list, 1)), ACT.Sigmoid)
+            gate[t] = new([P, N], F32, f"gate{t}")
+            cols = Z_CHUNKS[0]
+            nc.scalar.activation(gate[t][:, cols], h_t[:].indirect(entries(n1_list, cols)), ACT.Sigmoid)
+
+        def late_gates(tiles):
+            cols = Z_CHUNKS[1]
+            for t in tiles:
+                nc.scalar.activation(gate[t][:, cols], h[t][:].indirect(entries(n1_list, cols)), ACT.Sigmoid)
+
+        late_gates((0, 1))
 
         cand_scale_picked = new([P, N], U8, "cand_scale_picked", tag="slot_a")
         nc.vector.tensor_copy(cand_scale_picked[:], x_scale_tab[:].indirect(cand_list[:]))
@@ -141,89 +149,104 @@ def tile_picked_pqcgmaxlse_none_po_kernel(
 
         ex = [new([P, N], F32, f"ex{t}") for t in range(PACK)]
         neg_s = [new([P, N], F32, f"neg_s{t}") for t in range(PACK)]
-        ex_again = [new([P, PACK, HALF], F32, f"ex_again{c}") for c in range(2)]
+        ex_again = [new([P, PACK, HALF], F32, f"ex_again{c}", tag=f"slot_y{1 - c}") for c in range(2)]
         s_bank = {}
-        for c in range(N // HALF):
-            cols = slice(c * HALF, (c + 1) * HALF)
-            z_planes = new([P, PACK, HALF], BF16, f"z_planes{c}", tag="slot_c" if c == 0 else "")
-            other_head = new([P, HALF], F32, f"other_head{c}")
-            other_rest = new([P, PACK - 1, HALF], F32, f"other_rest{c}", tag="slot_c" if c == 1 else "")
-            gated_head = new([P, HALF], F32, f"gated_head{c}")
-            gated_rest = new([P, PACK - 1, HALF], F32, f"gated_rest{c}", tag="slot_d" if c == 1 else "")
-            other = [other_head[:]] + [other_rest[:, t, :] for t in range(PACK - 1)]
-            gated = [gated_head[:]] + [gated_rest[:, t, :] for t in range(PACK - 1)]
-            for t in range(PACK + 1):
-                if t < PACK:
-                    nc.vector.tensor_tensor(gated[t], h[t][:, cols], gate[c, t][:], ALU.mult)
-                if t > 0:
-                    larger = new([P, HALF], F32, f"larger{c}{t}")
-                    nc.vector.tensor_tensor(larger[:], gated[t - 1], other[t - 1], ALU.max)
-                    nc.scalar.activation(z_planes[:, t - 1, :], larger[:], ACT.Copy, scale=gain[:, t - 1 : t])
-                if t < PACK:
-                    nc.vector.tensor_copy(other[t], h[t][:].indirect(half_of(n2_list, c)))
-            z_woven = new([P, PACK * HALF], BF16, f"z_woven{c}", tag="slot_d" if c == 0 else "")
-            dst, src = weave_views(z_woven[:], z_planes[:])
-            nc.vector.tensor_copy(dst, src)
-            z_words = new([P, HALF], U32, f"z_words{c}")
-            z_scales = new([P, HALF], U8, f"z_scales{c}")
-            nc.vector.quantize_mx(out=z_words[:].bitcast(FP8X4), scales=z_scales[:], in_=z_woven[:])
-            for pair in range(2):
-                bank = psum.tile([P, 2, HALF], F32, name=f"s_bank{c}{pair}")
-                s_bank[c, pair] = bank
-                for u in range(2):
-                    t = 2 * pair + u
-                    rows = slice(t * P, (t + 1) * P)
+        for c, cols in enumerate(Z_CHUNKS):
+            width = cols.stop - cols.start
+            last = c == len(Z_CHUNKS) - 1
+            pieces = [slice(0, HALF), slice(HALF, width)] if width > HALF else [slice(0, width)]
+            gated = new([P, PACK, width], F32, f"gated{c}", tag="slot_c")
+            larger = new([P, PACK, width], F32, f"larger{c}")
+            z_woven = new([P, PACK * width], BF16, f"z_woven{c}", tag="" if last else "slot_e")
+            if last:
+                for pair, slot in enumerate(("slot_d", "slot_e")):
+                    other = new([P, 2, width], F32, f"other_pair{pair}", tag=slot)
+                    for t in (2 * pair, 2 * pair + 1):
+                        nc.vector.tensor_tensor(gated[:, t, :], h[t][:, cols], gate[t][:, cols], ALU.mult)
+                    for u in range(2):
+                        nc.vector.tensor_copy(other[:, u, :], h[2 * pair + u][:].indirect(entries(n2_list, cols)))
+                    both = slice(2 * pair, 2 * pair + 2)
+                    nc.vector.tensor_tensor(larger[:, both, :], gated[:, both, :], other[:], ALU.max)
+                dst, src = weave_views(z_woven[:], larger[:])
+                spread = gain[:].unsqueeze(1).unsqueeze(3).broadcast_to([P, width // 4, PACK, 4])
+                nc.vector.tensor_tensor(dst, src, spread, ALU.mult)
+            else:
+                other = new([P, PACK, width], F32, "other", tag="slot_d")
+                z_planes = new([P, PACK, width], BF16, "z_planes")
+                for t in range(PACK + 1):
+                    if t < PACK:
+                        nc.vector.tensor_tensor(gated[:, t, :], h[t][:, cols], gate[t][:, cols], ALU.mult)
+                    if t > 0:
+                        u = t - 1
+                        nc.vector.tensor_tensor(larger[:, u, :], gated[:, u, :], other[:, u, :], ALU.max)
+                        nc.scalar.activation(z_planes[:, u, :], larger[:, u, :], ACT.Copy, scale=gain[:, u:t])
+                    if t < PACK:
+                        for piece in pieces:
+                            nc.vector.tensor_copy(other[:, t, piece], h[t][:].indirect(entries(n2_list, piece)))
+                dst, src = weave_views(z_woven[:], z_planes[:])
+                nc.scalar.copy(dst, src)
+                late_gates((2, 3))
+            z_words = new([P, width], U32, f"z_words{c}")
+            z_scales = new([P, width], U8, f"z_scales{c}")
+            for piece in pieces:
+                nc.vector.quantize_mx(
+                    out=z_words[:, piece].bitcast(FP8X4),
+                    scales=z_scales[:, piece],
+                    in_=z_woven[:, PACK * piece.start : PACK * piece.stop],
+                )
+            for t in range(PACK):
+                rows = slice(t * P, (t + 1) * P)
+                bank = psum.tile([P, width], F32, name=f"s_bank{c}{t}", tag=f"h_bank{t}" if last else "")
+                s_bank[c, t] = bank
+                for piece in pieces:
                     nc.tensor.matmul_mx(
-                        out=bank[:, u, :],
+                        out=bank[:, piece],
                         lhsT=cand_words[:, rows].bitcast(FP8X4),
                         lhsT_scale=cand_scales[:, rows],
-                        rhs=z_words[:].bitcast(FP8X4),
-                        rhs_scale=z_scales[:],
+                        rhs=z_words[:, piece].bitcast(FP8X4),
+                        rhs_scale=z_scales[:, piece],
                         start=True,
                         stop=True,
                     )
-                for u in range(2):
-                    t = 2 * pair + u
-                    nc.scalar.activation(ex[t][:, cols], bank[:, u, :], ACT.Exp, scale=0.0625)
-                    if c == 0:
-                        nc.sync.dma_start(ex_again[c][:, t, :], ex[t][:, cols])
-                    else:
-                        nc.vector.tensor_copy(ex_again[c][:, t, :], ex[t][:, cols])
+                nc.scalar.activation(ex[t][:, cols], bank[:], ACT.Exp, scale=0.0625)
+                nc.sync.dma_start(ex_again[c][:, t, :], ex[t][:, cols])
 
-        for c in range(N // HALF):
-            cols = slice(c * HALF, (c + 1) * HALF)
-            for t in range(PACK):
-                nc.scalar.activation(neg_s[t][:, cols], s_bank[c, t // 2][:, t % 2, :], ACT.Copy, scale=-0.0625)
-
+        warm_ln = new([P, 1], F32, "warm_ln")
+        nc.scalar.activation(warm_ln[:], ex[PACK - 1][:, N - 1 : N], ACT.Ln)
         log_sum = []
-        for c in range(N // HALF):
+        for c, cols in enumerate(Z_CHUNKS):
             pair_sum = new([P, PACK, HALF], F32, f"pair_sum{c}")
             for t in range(PACK):
                 nc.vector.tensor_tensor(
-                    pair_sum[:, t, :], ex[t][:].indirect(half_of(n3_list, c)), ex_again[c][:, t, :], ALU.add
+                    pair_sum[:, t, :], ex[t][:].indirect(entries(n3_list, cols)), ex_again[c][:, t, :], ALU.add
                 )
             log_c = new([P, PACK, HALF], F32, f"log_sum{c}")
             nc.scalar.activation(log_c[:], pair_sum[:], ACT.Ln)
             log_sum.append(log_c)
+            if c == 0:
+                for half, places in enumerate(Z_CHUNKS):
+                    for t in range(PACK):
+                        nc.scalar.activation(neg_s[t][:, places], s_bank[half, t][:], ACT.Copy, scale=-0.0625)
 
         out_rows = out_0.rearrange("(p t) j -> p t j", t=PACK)
         out_words = out_1[0].rearrange("p n t -> p (n t)").bitcast(I32)
         y_scales = new([P, N], U8, "y_scales")
-        for c in range(N // HALF):
-            cols = slice(c * HALF, (c + 1) * HALF)
-            y = new([P, PACK, HALF], F32, f"y{c}")
+        for c, cols in enumerate(Y_CHUNKS):
+            width = cols.stop - cols.start
+            within = slice(cols.start % HALF, cols.start % HALF + width)
+            y = new([P, PACK, width], F32, f"y{c}", tag=f"slot_y{c}")
             for t in range(PACK):
                 nc.vector.tensor_tensor(
-                    y[:, t, :], neg_s[t][:].indirect(half_of(n4_list, c)), log_sum[c][:, t, :], ALU.add
+                    y[:, t, :], neg_s[t][:].indirect(entries(n4_list, cols)), log_sum[cols.start // HALF][:, t, within], ALU.add
                 )
             nc.sync.dma_start(out_rows[:, :, cols], y[:])
-            y_woven = new([P, PACK * HALF], BF16, f"y_woven{c}")
+            y_woven = new([P, PACK * width], BF16, f"y_woven{c}")
             dst, src = weave_views(y_woven[:], y[:])
-            if c == 0:
+            if c < len(Y_CHUNKS) - 1:
                 nc.scalar.copy(dst, src)
             else:
                 nc.vector.tensor_copy(dst, src)
-            y_words = new([P, HALF], U32, f"y_words{c}")
+            y_words = new([P, width], U32, f"y_words{c}")
             nc.vector.quantize_mx(out=y_words[:].bitcast(FP8X4), scales=y_scales[:, cols], in_=y_woven[:])
             nc.sync.dma_start(out_words[:, cols], y_words[:].bitcast(I32))
         for q in range(4):

@@ -104,10 +104,15 @@ def tile_picked_pqcgmaxlse_none_po_kernel(
         place_scale_rows(nc.scalar, first_scales, first_staged)
         tok_words = new([P, N], U32, "tok_words")
         nc.vector.tensor_copy(tok_words[:], x_word_tab[:].bitcast(U32).indirect(offs_list[:]))
-        dict_picked = new([P, N], U32, "dict_picked", tag="slot_a")
-        nc.vector.tensor_copy(dict_picked[:], d_word_tab[:].bitcast(U32).indirect(k1_list[:]))
         dict_words = new([P, N], U32, "dict_words")
-        deal(dict_words[:], dict_picked[:])
+        dict_picked = [new([P, HALF], U32, f"dict_picked{c}", tag=f"slot_a{c}") for c in range(2)]
+        for c, cols in enumerate(Z_CHUNKS):
+            nc.vector.tensor_copy(dict_picked[c][:], d_word_tab[:].bitcast(U32).indirect(entries(k1_list, cols)))
+        for c in range(2):
+            nc.vector.tensor_copy(
+                dict_words[:].rearrange("p (t m) -> p m t", t=PACK)[:, 64 * c : 64 * c + 64, :],
+                dict_picked[c][:].rearrange("p (m t) -> p m t", t=PACK),
+            )
 
         h = []
         gate = {}
@@ -135,9 +140,9 @@ def tile_picked_pqcgmaxlse_none_po_kernel(
             for t in tiles:
                 nc.scalar.activation(gate[t][:, cols], h[t][:].indirect(entries(n1_list, cols)), ACT.Sigmoid)
 
-        late_gates((0, 1))
+        late_gates((0, 1, 2, 3))
 
-        cand_scale_picked = new([P, N], U8, "cand_scale_picked", tag="slot_a")
+        cand_scale_picked = new([P, N], U8, "cand_scale_picked", tag="slot_a0")
         nc.vector.tensor_copy(cand_scale_picked[:], x_scale_tab[:].indirect(cand_list[:]))
         cand_picked = new([P, N], U32, "cand_picked", tag="slot_b")
         nc.vector.tensor_copy(cand_picked[:], x_word_tab[:].bitcast(U32).indirect(cand_list[:]))
@@ -151,6 +156,7 @@ def tile_picked_pqcgmaxlse_none_po_kernel(
         neg_s = [new([P, N], F32, f"neg_s{t}") for t in range(PACK)]
         ex_again = [new([P, PACK, HALF], F32, f"ex_again{c}", tag=f"slot_y{1 - c}") for c in range(2)]
         s_bank = {}
+        z_codes = []
         for c, cols in enumerate(Z_CHUNKS):
             width = cols.stop - cols.start
             last = c == len(Z_CHUNKS) - 1
@@ -158,6 +164,7 @@ def tile_picked_pqcgmaxlse_none_po_kernel(
             gated = new([P, PACK, width], F32, f"gated{c}", tag="slot_c")
             larger = new([P, PACK, width], F32, f"larger{c}")
             z_woven = new([P, PACK * width], BF16, f"z_woven{c}", tag="" if last else "slot_e")
+            z_planes = new([P, PACK, width], BF16, f"z_planes{c}")
             if last:
                 for pair, slot in enumerate(("slot_d", "slot_e")):
                     other = new([P, 2, width], F32, f"other_pair{pair}", tag=slot)
@@ -166,26 +173,34 @@ def tile_picked_pqcgmaxlse_none_po_kernel(
                     for u in range(2):
                         nc.vector.tensor_copy(other[:, u, :], h[2 * pair + u][:].indirect(entries(n2_list, cols)))
                     both = slice(2 * pair, 2 * pair + 2)
-                    nc.vector.tensor_tensor(larger[:, both, :], gated[:, both, :], other[:], ALU.max)
-                dst, src = weave_views(z_woven[:], larger[:])
-                spread = gain[:].unsqueeze(1).unsqueeze(3).broadcast_to([P, width // 4, PACK, 4])
-                nc.vector.tensor_tensor(dst, src, spread, ALU.mult)
+                    if pair == 0:
+                        nc.vector.tensor_tensor(larger[:, both, :], gated[:, both, :], other[:], ALU.max)
+                    else:
+                        for u in range(2):
+                            nc.vector.tensor_tensor(larger[:, 2 + u, :], gated[:, 2 + u, :], other[:, u, :], ALU.max)
+                    for t in (2 * pair, 2 * pair + 1):
+                        if pair == 0:
+                            nc.scalar.activation(
+                                z_planes[:, t, :], larger[:, t, :], ACT.Copy, scale=gain[:, t : t + 1]
+                            )
+                        else:
+                            nc.vector.tensor_scalar(
+                                z_planes[:, t, :], larger[:, t, :], gain[:, t : t + 1], None, ALU.mult
+                            )
+                pieces = [slice(0, P), slice(P, width)]
+                for piece in pieces:
+                    dst, src = weave_views(z_woven[:, PACK * piece.start : PACK * piece.stop], z_planes[:, :, piece])
+                    nc.vector.tensor_copy(dst, src)
             else:
                 other = new([P, PACK, width], F32, "other", tag="slot_d")
-                z_planes = new([P, PACK, width], BF16, "z_planes")
-                for t in range(PACK + 1):
-                    if t < PACK:
-                        nc.vector.tensor_tensor(gated[:, t, :], h[t][:, cols], gate[t][:, cols], ALU.mult)
-                    if t > 0:
-                        u = t - 1
-                        nc.vector.tensor_tensor(larger[:, u, :], gated[:, u, :], other[:, u, :], ALU.max)
-                        nc.scalar.activation(z_planes[:, u, :], larger[:, u, :], ACT.Copy, scale=gain[:, u:t])
-                    if t < PACK:
-                        for piece in pieces:
-                            nc.vector.tensor_copy(other[:, t, piece], h[t][:].indirect(entries(n2_list, piece)))
+                for t in range(PACK):
+                    nc.vector.tensor_copy(other[:, t, :], h[t][:].indirect(entries(n2_list, cols)))
+                    nc.vector.tensor_tensor(gated[:, t, :], h[t][:, cols], gate[t][:, cols], ALU.mult)
+                nc.vector.tensor_tensor(larger[:], gated[:], other[:], ALU.max)
+                for t in range(PACK):
+                    nc.scalar.activation(z_planes[:, t, :], larger[:, t, :], ACT.Copy, scale=gain[:, t : t + 1])
                 dst, src = weave_views(z_woven[:], z_planes[:])
                 nc.scalar.copy(dst, src)
-                late_gates((2, 3))
             z_words = new([P, width], U32, f"z_words{c}")
             z_scales = new([P, width], U8, f"z_scales{c}")
             for piece in pieces:
@@ -194,6 +209,13 @@ def tile_picked_pqcgmaxlse_none_po_kernel(
                     scales=z_scales[:, piece],
                     in_=z_woven[:, PACK * piece.start : PACK * piece.stop],
                 )
+            z_codes.append((z_words, z_scales))
+
+        for c, cols in enumerate(Z_CHUNKS):
+            width = cols.stop - cols.start
+            last = c == len(Z_CHUNKS) - 1
+            pieces = [slice(0, width)]
+            z_words, z_scales = z_codes[c]
             for t in range(PACK):
                 rows = slice(t * P, (t + 1) * P)
                 bank = psum.tile([P, width], F32, name=f"s_bank{c}{t}", tag=f"h_bank{t}" if last else "")

from contextlib import ExitStack

import concourse.mybir as mybir

F32 = mybir.dt.float32
BF16 = mybir.dt.bfloat16
U32 = mybir.dt.uint32
I32 = mybir.dt.int32
U16 = mybir.dt.uint16
U8 = mybir.dt.uint8
FP8X4 = mybir.dt.float8_e4m3fn_x4
ACT = mybir.ActivationFunctionType
ALU = mybir.AluOpType

P = 128
PACK = 4
T, G, N = 1024, 2048, 512
HALF = 256
WIDE = 2 * N
Z_CHUNKS = (slice(0, 256), slice(256, 512))
Y_CHUNKS = (slice(0, 256), slice(256, 384), slice(384, 512))
LIST_COLS = N // 16
FLOPS = 2 * 2 * 512 * 512 * 512


def tile_picked_pqcgmaxlse_none_po_kernel(
    tc, x_words, x_scales, d_words, d_scales, gs, offs, k1, n1, n2, cand, n3, n4, out_0, out_1, out_2
):
    nc = tc.nc
    with ExitStack() as ctx:
        keep = ctx.enter_context(tc.tile_pool(name="keep", bufs=1))
        psum = ctx.enter_context(tc.psum_pool(name="psum", bufs=1))

        def new(shape, dtype, name, tag=""):
            return keep.tile(shape, dtype, name=name, tag=tag, align_bytes=64)

        def load_list(src, name):
            tile = keep.tile([P, LIST_COLS], U16, name=name)
            nc.sync.dma_start(tile[:], src)
            return tile

        def load_scale_rows(src, width, name):
            tile = new([P, width], U8, name)
            rows = src[0].bitcast(I32).unsqueeze(1).broadcast_to([16, 8, width // 4])
            nc.sync.dma_start(tile[:].bitcast(I32), rows)
            return tile

        def load_words(src, width, name):
            tile = new([P, width], I32, name)
            nc.sync.dma_start(tile[:], src[0].rearrange("p n t -> p (n t)").bitcast(I32))
            return tile

        def place_scale_rows(queue, dst, src):
            for q in range(4):
                queue.dma_start(
                    dst[32 * q : 32 * q + 4, :].bitcast(I32), src[32 * q : 32 * q + 32 : 8, :].bitcast(I32)
                )

        def deal(dst, src):
            nc.vector.tensor_copy(
                dst.rearrange("p (t m) -> p m t", t=PACK), src.rearrange("p (m t) -> p m t", t=PACK)
            )

        def entries(lst, cols):
            return lst[:, cols.start // 16 : cols.stop // 16]

        def weave_views(woven, planes):
            return (
                woven.rearrange("p (c i t) -> p c t i", i=4, t=PACK),
                planes.rearrange("p t (c i) -> p c t i", i=4),
            )

        x_scale_tab = load_scale_rows(x_scales, T, "x_scale_tab")
        offs_list = load_list(offs, "offs_list")
        d_scale_tab = load_scale_rows(d_scales, G, "d_scale_tab")
        k1_list = load_list(k1, "k1_list")
        x_word_tab = load_words(x_words, T, "x_word_tab")
        d_word_tab = load_words(d_words, G, "d_word_tab")
        cand_list = load_list(cand, "cand_list")
        n1_list = load_list(n1, "n1_list")
        n2_list = load_list(n2, "n2_list")
        gain = new([P, PACK], F32, "gain")
        nc.sync.dma_start(gain[:], gs.rearrange("(p t) o -> p (t o)", t=PACK))
        n3_list = load_list(n3, "n3_list")
        n4_list = load_list(n4, "n4_list")

        warm = new([P, 1], F32, "warm")
        nc.vector.memset(warm[:], 0.0)
        warm_out = new([P, 1], F32, "warm_out")
        nc.scalar.activation(warm_out[:], warm[:], ACT.Sigmoid)

        first_scales = new([P, 2 * N], U8, "first_scales")
        nc.vector.memset(first_scales[:].bitcast(I32), 0)
        cand_scales = new([P, N], U8, "cand_scales")
        nc.vector.memset(cand_scales[:].bitcast(I32), 0)

        tok_scale_picked = new([P, N], U8, "tok_scale_picked")
        nc.vector.tensor_copy(tok_scale_picked[:], x_scale_tab[:].indirect(offs_list[:]))
        dict_scale_picked = new([P, N], U8, "dict_scale_picked")
        nc.vector.tensor_copy(dict_scale_picked[:], d_scale_tab[:].indirect(k1_list[:]))
        first_staged = new([P, 2 * N], U8, "first_staged", tag="slot_b")
        nc.vector.tensor_copy(first_staged[:, N : 2 * N].bitcast(I32), tok_scale_picked[:].bitcast(I32))
        deal(first_staged[:, 0:N], dict_scale_picked[:])
        place_scale_rows(nc.scalar, first_scales, first_staged)
        tok_words = new([P, N], U32, "tok_words")
        nc.vector.tensor_copy(tok_words[:], x_word_tab[:].bitcast(U32).indirect(offs_list[:]))
        dict_words = new([P, N], U32, "dict_words")
        dict_picked = [new([P, HALF], U32, f"dict_picked{c}", tag=f"slot_a{c}") for c in range(2)]
        for c, cols in enumerate(Z_CHUNKS):
            nc.vector.tensor_copy(dict_picked[c][:], d_word_tab[:].bitcast(U32).indirect(entries(k1_list, cols)))
        for c in range(2):
            nc.vector.tensor_copy(
                dict_words[:].rearrange("p (t m) -> p m t", t=PACK)[:, 64 * c : 64 * c + 64, :],
                dict_picked[c][:].rearrange("p (m t) -> p m t", t=PACK),
            )

        h = []
        gate = {}
        for t in range(PACK):
            cols = slice(t * P, (t + 1) * P)
            bank = psum.tile([P, N], F32, name=f"h_bank{t}")
            nc.tensor.matmul_mx(
                out=bank[:],
                lhsT=dict_words[:, cols].bitcast(FP8X4),
                lhsT_scale=first_scales[:, cols],
                rhs=tok_words[:].bitcast(FP8X4),
                rhs_scale=first_scales[:, N : 2 * N],
                start=True,
                stop=True,
            )
            h_t = new([P, N], F32, f"h{t}")
            nc.scalar.activation(h_t[:], bank[:], ACT.Copy, scale=0.0625)
            h.append(h_t)
            gate[t] = new([P, N], F32, f"gate{t}")
            cols = Z_CHUNKS[0]
            nc.scalar.activation(gate[t][:, cols], h_t[:].indirect(entries(n1_list, cols)), ACT.Sigmoid)

        def late_gates(tiles):
            cols = Z_CHUNKS[1]
            for t in tiles:
                nc.scalar.activation(gate[t][:, cols], h[t][:].indirect(entries(n1_list, cols)), ACT.Sigmoid)

        late_gates((0, 1, 2, 3))

        cand_scale_picked = new([P, N], U8, "cand_scale_picked", tag="slot_a0")
        nc.vector.tensor_copy(cand_scale_picked[:], x_scale_tab[:].indirect(cand_list[:]))
        cand_picked = new([P, N], U32, "cand_picked", tag="slot_b")
        nc.vector.tensor_copy(cand_picked[:], x_word_tab[:].bitcast(U32).indirect(cand_list[:]))
        cand_staged = new([P, N], U8, "cand_staged")
        deal(cand_staged[:], cand_scale_picked[:])
        place_scale_rows(nc.sync, cand_scales, cand_staged)
        cand_words = new([P, N], U32, "cand_words")
        deal(cand_words[:], cand_picked[:])

        ex = [new([P, N], F32, f"ex{t}") for t in range(PACK)]
        neg_s = [new([P, N], F32, f"neg_s{t}") for t in range(PACK)]
        ex_again = [new([P, PACK, HALF], F32, f"ex_again{c}", tag=f"slot_y{1 - c}") for c in range(2)]
        s_bank = {}
        z_codes = []
        for c, cols in enumerate(Z_CHUNKS):
            width = cols.stop - cols.start
            last = c == len(Z_CHUNKS) - 1
            pieces = [slice(0, HALF), slice(HALF, width)] if width > HALF else [slice(0, width)]
            gated = new([P, PACK, width], F32, f"gated{c}", tag="slot_c")
            larger = new([P, PACK, width], F32, f"larger{c}")
            z_woven = new([P, PACK * width], BF16, f"z_woven{c}", tag="" if last else "slot_e")
            z_planes = new([P, PACK, width], BF16, f"z_planes{c}")
            if last:
                for pair, slot in enumerate(("slot_d", "slot_e")):
                    other = new([P, 2, width], F32, f"other_pair{pair}", tag=slot)
                    for t in (2 * pair, 2 * pair + 1):
                        nc.vector.tensor_tensor(gated[:, t, :], h[t][:, cols], gate[t][:, cols], ALU.mult)
                    for u in range(2):
                        nc.vector.tensor_copy(other[:, u, :], h[2 * pair + u][:].indirect(entries(n2_list, cols)))
                    both = slice(2 * pair, 2 * pair + 2)
                    if pair == 0:
                        nc.vector.tensor_tensor(larger[:, both, :], gated[:, both, :], other[:], ALU.max)
                    else:
                        for u in range(2):
                            nc.vector.tensor_tensor(larger[:, 2 + u, :], gated[:, 2 + u, :], other[:, u, :], ALU.max)
                    for t in (2 * pair, 2 * pair + 1):
                        if pair == 0:
                            nc.scalar.activation(
                                z_planes[:, t, :], larger[:, t, :], ACT.Copy, scale=gain[:, t : t + 1]
                            )
                        else:
                            nc.vector.tensor_scalar(
                                z_planes[:, t, :], larger[:, t, :], gain[:, t : t + 1], None, ALU.mult
                            )
                pieces = [slice(0, P), slice(P, width)]
                for piece in pieces:
                    dst, src = weave_views(z_woven[:, PACK * piece.start : PACK * piece.stop], z_planes[:, :, piece])
                    nc.vector.tensor_copy(dst, src)
            else:
                other = new([P, PACK, width], F32, "other", tag="slot_d")
                for t in range(PACK):
                    nc.vector.tensor_copy(other[:, t, :], h[t][:].indirect(entries(n2_list, cols)))
                    nc.vector.tensor_tensor(gated[:, t, :], h[t][:, cols], gate[t][:, cols], ALU.mult)
                nc.vector.tensor_tensor(larger[:], gated[:], other[:], ALU.max)
                for t in range(PACK):
                    nc.scalar.activation(z_planes[:, t, :], larger[:, t, :], ACT.Copy, scale=gain[:, t : t + 1])
                dst, src = weave_views(z_woven[:], z_planes[:])
                nc.scalar.copy(dst, src)
            z_words = new([P, width], U32, f"z_words{c}")
            z_scales = new([P, width], U8, f"z_scales{c}")
            for piece in pieces:
                nc.vector.quantize_mx(
                    out=z_words[:, piece].bitcast(FP8X4),
                    scales=z_scales[:, piece],
                    in_=z_woven[:, PACK * piece.start : PACK * piece.stop],
                )
            z_codes.append((z_words, z_scales))

        for c, cols in enumerate(Z_CHUNKS):
            width = cols.stop - cols.start
            last = c == len(Z_CHUNKS) - 1
            pieces = [slice(0, width)]
            z_words, z_scales = z_codes[c]
            for t in range(PACK):
                rows = slice(t * P, (t + 1) * P)
                bank = psum.tile([P, width], F32, name=f"s_bank{c}{t}", tag=f"h_bank{t}" if last else "")
                s_bank[c, t] = bank
                for piece in pieces:
                    nc.tensor.matmul_mx(
                        out=bank[:, piece],
                        lhsT=cand_words[:, rows].bitcast(FP8X4),
                        lhsT_scale=cand_scales[:, rows],
                        rhs=z_words[:, piece].bitcast(FP8X4),
                        rhs_scale=z_scales[:, piece],
                        start=True,
                        stop=True,
                    )
                nc.scalar.activation(ex[t][:, cols], bank[:], ACT.Exp, scale=0.0625)
                nc.sync.dma_start(ex_again[c][:, t, :], ex[t][:, cols])

        warm_ln = new([P, 1], F32, "warm_ln")
        nc.scalar.activation(warm_ln[:], ex[PACK - 1][:, N - 1 : N], ACT.Ln)
        log_sum = []
        for c, cols in enumerate(Z_CHUNKS):
            pair_sum = new([P, PACK, HALF], F32, f"pair_sum{c}")
            for t in range(PACK):
                nc.vector.tensor_tensor(
                    pair_sum[:, t, :], ex[t][:].indirect(entries(n3_list, cols)), ex_again[c][:, t, :], ALU.add
                )
            log_c = new([P, PACK, HALF], F32, f"log_sum{c}")
            nc.scalar.activation(log_c[:], pair_sum[:], ACT.Ln)
            log_sum.append(log_c)
            if c == 0:
                for half, places in enumerate(Z_CHUNKS):
                    for t in range(PACK):
                        nc.scalar.activation(neg_s[t][:, places], s_bank[half, t][:], ACT.Copy, scale=-0.0625)

        out_rows = out_0.rearrange("(p t) j -> p t j", t=PACK)
        out_words = out_1[0].rearrange("p n t -> p (n t)").bitcast(I32)
        y_scales = new([P, N], U8, "y_scales")
        for c, cols in enumerate(Y_CHUNKS):
            width = cols.stop - cols.start
            within = slice(cols.start % HALF, cols.start % HALF + width)
            y = new([P, PACK, width], F32, f"y{c}", tag=f"slot_y{c}")
            for t in range(PACK):
                nc.vector.tensor_tensor(
                    y[:, t, :], neg_s[t][:].indirect(entries(n4_list, cols)), log_sum[cols.start // HALF][:, t, within], ALU.add
                )
            nc.sync.dma_start(out_rows[:, :, cols], y[:])
            y_woven = new([P, PACK * width], BF16, f"y_woven{c}")
            dst, src = weave_views(y_woven[:], y[:])
            if c < len(Y_CHUNKS) - 1:
                nc.scalar.copy(dst, src)
            else:
                nc.vector.tensor_copy(dst, src)
            y_words = new([P, width], U32, f"y_words{c}")
            nc.vector.quantize_mx(out=y_words[:].bitcast(FP8X4), scales=y_scales[:, cols], in_=y_woven[:])
            nc.sync.dma_start(out_words[:, cols], y_words[:].bitcast(I32))
        for q in range(4):
            queue = nc.sync if q % 2 == 0 else nc.scalar
            queue.dma_start(
                out_2[0].bitcast(I32)[4 * q : 4 * q + 4, :], y_scales[32 * q : 32 * q + 4, :].bitcast(I32)
            )
